import numpy as np
import ml_dtypes


def mxq(x, axis, fmt="e4m3"):
    dtype, down = {"e4m3": (ml_dtypes.float8_e4m3fn, 7), "e5m2": (ml_dtypes.float8_e5m2, 14)}[fmt]
    v = np.moveaxis(np.asarray(x, np.float32).astype(ml_dtypes.bfloat16).astype(np.float64), axis, -1)
    blocks = v.reshape(v.shape[:-1] + (-1, 32))
    amax = np.abs(blocks).max(-1, keepdims=True)
    byte = np.maximum(np.where(amax > 0, np.frexp(amax)[1] - 1 + 127, 0) - down, 1)
    scale = np.exp2(byte - 127.0)
    codes = (blocks / scale).astype(np.float32).astype(dtype).astype(np.float64)
    return np.moveaxis((codes * scale).reshape(v.shape), -1, axis)


WIDE = False


def mx_kscale(k):
    if not WIDE:
        return np.ones(k)
    levels = np.array([30, -30])
    if k % 512:
        return np.exp2(np.random.permutation(np.resize(levels, k // 32))).repeat(32)
    a = np.empty((k // 512, 16))
    for p in range(k // 512):
        a[p, :8] = np.random.permutation(np.resize(levels, 8))
        for g in range(8):
            far = levels[np.abs(levels - a[p, g]) >= 10]
            a[p, g + 8] = far[np.random.randint(len(far))]
    return np.exp2(a.ravel()).repeat(32)


def f64(x):
    return np.asarray(x).astype(np.float64)


def striped(idx):
    return np.tile(np.asarray(idx).reshape(-1, 16).T, (8, 1)).astype(np.uint16)


def unstriped(offs):
    return offs[:16].T.reshape(-1).astype(np.int64)


E2M1 = np.array([0.0, 0.5, 1.0, 1.5, 2.0, 3.0, 4.0, 6.0, -0.0, -0.5, -1.0, -1.5, -2.0, -3.0, -4.0, -6.0])


def pack_weight(w, fmt):
    k, n = w.shape
    w = f64(np.asarray(w, np.float32).astype(ml_dtypes.bfloat16)).reshape(k // 32, 32, n)
    amax = np.abs(w).max(1)
    if fmt in ("e4m3", "e5m2"):
        byte = np.frexp(amax)[1] - 1 + 127 - (7 if fmt == "e4m3" else 14)
    else:
        mant, ex = np.frexp(amax / 6.0)
        byte = np.where(mant > 0.5, ex, ex - 1) + 127
    byte = np.clip(np.where(amax > 0, byte, 1), 1, 254)
    scaled = (w * np.exp2(127.0 - byte)[:, None, :]).reshape(k, n).astype(np.float32)
    by_word = np.ascontiguousarray(scaled.reshape(k // 512, 128, 4, n).transpose(0, 1, 3, 2))
    if fmt in ("e4m3", "e5m2"):
        words = by_word.astype(ml_dtypes.float8_e4m3fn if fmt == "e4m3" else ml_dtypes.float8_e5m2).view(np.uint8)
    else:
        c = by_word.astype(ml_dtypes.float4_e2m1fn).view(np.uint8) & 0xF
        words = (c[..., 0::2] | (c[..., 1::2] << 4)).reshape(k // 512, 128, 2 * n)
    return np.ascontiguousarray(words), np.ascontiguousarray(byte.astype(np.uint8).reshape(k // 512, 16, n))


def unpack_weight(words, scales, fmt):
    g, _, n = scales.shape
    words = np.ascontiguousarray(words).reshape(g, 128, n, -1)
    if fmt in ("e4m3", "e5m2"):
        vals = words.view(ml_dtypes.float8_e4m3fn if fmt == "e4m3" else ml_dtypes.float8_e5m2).astype(np.float64)
    else:
        nib = np.empty((g, 128, n, 4), np.uint8)
        nib[..., 0::2] = words & 0xF
        nib[..., 1::2] = words >> 4
        vals = E2M1[nib]
    vals = vals * np.repeat(np.exp2(scales.astype(np.float64) - 127.0), 8, axis=1)[..., None]
    return vals.transpose(0, 1, 3, 2).reshape(g * 512, n)


K, T, J, R, C, O, N = 512, 1024, 256, 512, 512, 128, 256


def setup_inputs():
    n = np.random.standard_normal
    idx = np.random.permutation(T)[:J]
    idx2 = np.random.permutation(C)[:J]
    idx3 = np.random.permutation(C)[:J]
    idx4 = np.random.permutation(J)[:O]
    idx5 = np.random.permutation(J)[:O]
    fk = mx_kscale(K)
    fr = mx_kscale(R)
    xtp = pack_weight(n((K, T)) / fk[:, None], "e5m2")
    wp = pack_weight(n((K, R)) * 1 / np.sqrt(K) * fk[:, None] * fr, "e2m1")
    w2p = pack_weight(n((K, R)) * 1 / np.sqrt(K) * fk[:, None] * fr, "e4m3")
    wbp = pack_weight(n((R, N)) * 1 / np.sqrt(R) / fr[:, None], "e2m1")
    return {
        "xt_words": xtp[0],
        "xt_scales": xtp[1],
        "w_words": wp[0],
        "w_scales": wp[1],
        "w2_words": w2p[0],
        "w2_scales": w2p[1],
        "sa": (np.random.uniform(0.5, 1.6, (R, 1))).astype(np.float32),
        "sb": (np.random.uniform(0.5, 1.6, (R, 1))).astype(np.float32),
        "wb_words": wbp[0],
        "wb_scales": wbp[1],
        "offs": striped(idx),
        "offs2": striped(idx2),
        "offs3": striped(idx3),
        "offs4": striped(idx4),
        "offs5": striped(idx5),
    }


def reference(xt_words, xt_scales, w_words, w_scales, w2_words, w2_scales, sa, sb, wb_words, wb_scales, offs, offs2, offs3, offs4, offs5):
    idx = unstriped(offs)
    idx2 = unstriped(offs2)
    idx3 = unstriped(offs3)
    idx4 = unstriped(offs4)
    idx5 = unstriped(offs5)
    xtu = unpack_weight(xt_words, xt_scales, "e5m2")
    wu = unpack_weight(w_words, w_scales, "e2m1")
    w2u = unpack_weight(w2_words, w2_scales, "e4m3")
    wbu = unpack_weight(wb_words, wb_scales, "e2m1")
    xtidxg = xtu[:, idx]
    a = wu.T @ xtidxg
    b = w2u.T @ xtidxg
    pw = np.zeros((R, C))
    pw[:, idx2] = a
    rb = np.maximum(pw[:, idx3] * f64(sa), b)
    hid = np.abs(rb[:, idx4] - rb[:, idx5] * f64(sb))
    hidq = mxq(hid, 0, "e4m3")
    y = wbu.T @ hidq
    return y

@@ -1,0 +1,231 @@
+from contextlib import ExitStack
+
+import concourse.mybir as mybir
+
+K, T, J, R, C, O, N = 512, 1024, 256, 512, 512, 128, 256
+FLOPS = 2 * K * R * J * 2 + 2 * R * N * O
+
+F32 = mybir.dt.float32
+BF16 = mybir.dt.bfloat16
+I32 = mybir.dt.int32
+U32 = mybir.dt.uint32
+U16 = mybir.dt.uint16
+U8 = mybir.dt.uint8
+E4M3 = mybir.dt.float8_e4m3fn_x4
+E5M2 = mybir.dt.float8_e5m2_x4
+E2M1 = mybir.dt.float4_e2m1fn_x4
+ALU = mybir.AluOpType
+ACT = mybir.ActivationFunctionType
+
+P = 128
+PACK = 4
+
+
+def load_scale_rows(queue, plane, scales, quadrants):
+    for q in quadrants:
+        queue.dma_start(
+            out=plane[32 * q : 32 * q + 4, :].bitcast(I32),
+            in_=scales[0, 4 * q : 4 * q + 4, :].bitcast(I32),
+        )
+
+
+def deal(engine, dealt, loaded, line, ts):
+    engine.tensor_copy(
+        out=dealt.rearrange("p (t c i) -> p c t i", t=PACK, i=line)[:, :, ts, :],
+        in_=loaded.rearrange("p (c i t) -> p c t i", t=PACK, i=line)[:, :, ts, :],
+    )
+
+
+def tile_list_boardanswer_twow_one_plain_kernel(
+    tc, xt_words, xt_scales, w_words, w_scales, w2_words, w2_scales, sa, sb, wb_words, wb_scales,
+    offs, offs2, offs3, offs4, offs5, out,
+):
+    nc = tc.nc
+    with ExitStack() as ctx:
+        keep = ctx.enter_context(tc.tile_pool(name="keep", bufs=1))
+        ring = ctx.enter_context(tc.tile_pool(name="ring", bufs=4))
+        psum = ctx.enter_context(tc.psum_pool(name="psum", bufs=1))
+
+        list1 = keep.tile([P, J // 16], U16, name="list1")
+        list2 = keep.tile([P, J // 16], U16, name="list2")
+        list3 = keep.tile([P, J // 16], U16, name="list3")
+        list4 = keep.tile([P, O // 16], U16, name="list4")
+        list5 = keep.tile([P, O // 16], U16, name="list5")
+
+        xt_w = keep.tile([P, T], U32, name="xt_w", align_bytes=64)
+        xt_s = keep.tile([P, T], U8, name="xt_s", align_bytes=64)
+        w_w = keep.tile([P, R], U16, name="w_w", align_bytes=64)
+        w_s = keep.tile([P, 4, R], U8, name="w_s", align_bytes=64)
+        w2_w = keep.tile([P, R], U32, name="w2_w", align_bytes=64)
+        w2_s = keep.tile([P, R], U8, name="w2_s", align_bytes=64)
+        wb_w = keep.tile([P, N], U16, name="wb_w", align_bytes=64)
+        wb_s = keep.tile([P, N], U8, name="wb_s", align_bytes=64)
+        sa_t = keep.tile([P, PACK], F32, name="sa_t")
+        sb_t = keep.tile([P, PACK], F32, name="sb_t")
+        boards = [keep.tile([P, C], F32, name=f"board{t}") for t in range(PACK)]
+
+        w_s_words = w_s[:].rearrange("p q c -> p (q c)").bitcast(I32)
+        row = R // 4
+        nc.vector.memset(w_s_words.rearrange("p (a b c) -> p a b c", a=2, b=2)[:, :, 0, :], 0)
+        nc.vector.memset(xt_s[:].bitcast(I32), 0)
+        for plane in (w2_s, wb_s):
+            nc.vector.memset(plane[:].bitcast(I32), 0)
+        for t in range(PACK):
+            nc.vector.memset(boards[t][:], 0.0)
+
+        nc.sync.dma_start(out=w_w[:].bitcast(I32), in_=w_words[0].bitcast(I32))
+        nc.scalar.dma_start(out=xt_w[:].bitcast(I32), in_=xt_words[0].rearrange("p n t -> p (n t)").bitcast(I32))
+        nc.sync.dma_start(
+            out=w_s_words[0:4, :].rearrange("r (q c) -> r q c", q=4),
+            in_=w_scales[0].bitcast(I32).rearrange("(q r) c -> r q c", r=4),
+        )
+        load_scale_rows(nc.sync, xt_s, xt_scales, range(4))
+        nc.sync.dma_start(list1[:], offs)
+        nc.gpsimd.dma_start(out=sa_t[:], in_=sa.rearrange("(p t) one -> p (t one)", t=PACK))
+        nc.gpsimd.dma_start(out=sb_t[:], in_=sb.rearrange("(p t) one -> p (t one)", t=PACK))
+        nc.sync.dma_start(list2[:], offs2)
+        nc.sync.dma_start(out=w2_w[:].bitcast(I32), in_=w2_words[0].rearrange("p n t -> p (n t)").bitcast(I32))
+        load_scale_rows(nc.sync, w2_s, w2_scales, range(4))
+        nc.sync.dma_start(list5[:], offs5)
+        nc.sync.dma_start(list4[:], offs4)
+        nc.sync.dma_start(list3[:], offs3)
+        nc.sync.dma_start(out=wb_w[:].bitcast(I32), in_=wb_words[0].bitcast(I32))
+        load_scale_rows(nc.sync, wb_s, wb_scales, range(4))
+
+        x_w = keep.tile([P, J], U32, name="x_w", align_bytes=64)
+        x_s = keep.tile([P, J], U8, name="x_s", align_bytes=64)
+        w_wd = keep.tile([P, R], U16, name="w_wd", align_bytes=64)
+        w_sd = keep.tile([P, R], U8, name="w_sd", align_bytes=64)
+        w2_wd = keep.tile([P, R], U32, name="w2_wd", align_bytes=64)
+        w2_sd = keep.tile([P, R], U8, name="w2_sd", align_bytes=64)
+
+        H = J // 2
+        deal(nc.vector, w_wd[:], w_w[:], 8, slice(0, 4))
+        nc.vector.tensor_copy(out=w_s_words[32:36, 0 : 3 * row], in_=w_s_words[0:4, row : 4 * row])
+        nc.vector.tensor_copy(out=w_s_words[64:128, 0:row], in_=w_s_words[0:64, 2 * row : 3 * row])
+        deal(nc.gpsimd, w_sd[:], w_s[:, 0, :], 16, slice(0, 2))
+        deal(nc.gpsimd, w_sd[:], w_s[:, 0, :], 16, slice(2, 4))
+        for h in range(2):
+            nc.vector.tensor_copy(x_s[:, h * H : (h + 1) * H], xt_s[:].indirect(list1[:, h * 8 : (h + 1) * 8]))
+            nc.vector.tensor_copy(x_w[:, h * H : (h + 1) * H], xt_w[:].indirect(list1[:, h * 8 : (h + 1) * 8]))
+        deal(nc.gpsimd, w2_wd[:], w2_w[:], 4, slice(0, 4))
+        deal(nc.gpsimd, w2_sd[:], w2_s[:], 16, slice(0, 4))
+
+        early_ps = [psum.tile([P, H], F32, name=f"early_ps{e}", tag=f"narrow{e}") for e in range(2)]
+        late_ps = [psum.tile([P, H], F32, name=f"late_ps{e}") for e in range(2)]
+        whole_ps = [psum.tile([P, J], F32, name=f"whole_ps{e}") for e in range(2)]
+        b_ps = [psum.tile([P, 2, J], F32, name=f"b_ps{h}") for h in range(2)]
+
+        def first_product(dst, t, lo, hi):
+            cols = slice(t * P, (t + 1) * P)
+            nc.tensor.matmul_mx(
+                out=dst, lhsT=w_wd[:, cols].bitcast(E2M1), lhsT_scale=w_sd[:, cols],
+                rhs=x_w[:, lo:hi].bitcast(E5M2), rhs_scale=x_s[:, lo:hi], start=True, stop=True,
+            )
+
+        first_product(early_ps[0][:], 0, 0, H)
+        first_product(early_ps[1][:], 1, 0, H)
+        first_product(late_ps[0][:], 0, H, J)
+        first_product(late_ps[1][:], 1, H, J)
+        first_product(whole_ps[0][:], 3, 0, J)
+        first_product(whole_ps[1][:], 2, 0, J)
+        for t in range(PACK):
+            cols = slice(t * P, (t + 1) * P)
+            nc.tensor.matmul_mx(
+                out=b_ps[t // 2][:, t % 2, :], lhsT=w2_wd[:, cols].bitcast(E4M3), lhsT_scale=w2_sd[:, cols],
+                rhs=x_w[:].bitcast(E5M2), rhs_scale=x_s[:], start=True, stop=True,
+            )
+
+        early_sb = [keep.tile([P, H], F32, name=f"early_sb{e}") for e in range(2)]
+        late_sb = [keep.tile([P, H + J], F32, name=f"late_sb{e}") for e in range(2)]
+        picked = {}
+        rb = [keep.tile([P, J], F32, name=f"rb{t}") for t in range(PACK)]
+        other = [keep.tile([P, O], F32, name=f"other{t}") for t in range(PACK)]
+        own = [keep.tile([P, O], F32, name=f"own{t}") for t in range(PACK)]
+        diff = keep.tile([P, PACK, O], F32, name="diff")
+
+        def put_scalar(t, lo, hi, values):
+            nc.scalar.activation(out=boards[t][:].indirect(list2[:, lo // 16 : hi // 16]), in_=values, func=ACT.Copy)
+
+        def put_vector(t, lo, hi, values):
+            nc.vector.tensor_copy(boards[t][:].indirect(list2[:, lo // 16 : hi // 16]), values)
+
+        def pick_board(t):
+            picked[t] = ring.tile([P, J], F32, name="picked")
+            nc.scalar.activation(
+                out=picked[t][:], in_=boards[t][:].indirect(list3[:]), func=ACT.Copy, scale=sa_t[:, t : t + 1]
+            )
+
+        def larger(t):
+            nc.vector.tensor_tensor(out=rb[t][:], in0=picked[t][:], in1=b_ps[t // 2][:, t % 2, :], op=ALU.max)
+
+        def pick_other(t):
+            nc.scalar.activation(
+                out=other[t][:], in_=rb[t][:].indirect(list5[:]), func=ACT.Copy, scale=sb_t[:, t : t + 1]
+            )
+
+        def pick_own(t):
+            nc.vector.tensor_copy(own[t][:], rb[t][:].indirect(list4[:]))
+
+        def subtract(engine, t):
+            engine.tensor_tensor(out=diff[:, t, :], in0=own[t][:], in1=other[t][:], op=ALU.subtract)
+
+        hid = keep.tile([P, O, PACK], BF16, name="hid", align_bytes=64)
+
+        by_place = diff[:].rearrange("p t o -> p o t")
+
+        def magnitude_scalar(places, ts):
+            nc.scalar.activation(out=hid[:, places, ts], in_=by_place[:, places, ts], func=ACT.Abs)
+
+        SPLIT = 128
+        nc.scalar.activation(out=early_sb[0][:], in_=early_ps[0][:], func=ACT.Copy)
+        nc.vector.tensor_copy(out=early_sb[1][:], in_=early_ps[1][:])
+        put_scalar(0, 0, H, early_sb[0][:])
+        put_vector(1, 0, H, early_sb[1][:])
+        for cols, banks in ((slice(0, H), late_ps), (slice(H, H + J), whole_ps)):
+            nc.scalar.activation(out=late_sb[0][:, cols], in_=banks[0][:], func=ACT.Copy)
+            nc.vector.tensor_copy(out=late_sb[1][:, cols], in_=banks[1][:])
+        put_scalar(0, H, J, late_sb[0][:, 0:H])
+        put_vector(1, H, J, late_sb[1][:, 0:H])
+        put_scalar(3, 0, SPLIT, late_sb[0][:, H : H + SPLIT])
+        put_vector(2, 0, J, late_sb[1][:, H : H + J])
+        put_vector(3, SPLIT, J, late_sb[0][:, H + SPLIT : H + J])
+        pick_board(0)
+        pick_board(1)
+        pick_board(2)
+        larger(0)
+        larger(1)
+        pick_other(0)
+        pick_own(0)
+        subtract(nc.gpsimd, 0)
+        pick_board(3)
+        larger(2)
+        pick_other(1)
+        pick_own(1)
+        subtract(nc.gpsimd, 1)
+        larger(3)
+        pick_other(2)
+        pick_own(2)
+        pick_other(3)
+        pick_own(3)
+        subtract(nc.vector, 2)
+        subtract(nc.vector, 3)
+        magnitude_scalar(slice(0, O), slice(0, 2))
+        magnitude_scalar(slice(0, O), slice(2, 4))
+
+        hid_w = keep.tile([P, O], U32, name="hid_w", align_bytes=64)
+        hid_s = keep.tile([P, O], U8, name="hid_s", align_bytes=64)
+        nc.vector.quantize_mx(out=hid_w[:].bitcast(E4M3), scales=hid_s[:], in_=hid[:].rearrange("p o t -> p (o t)"))
+
+        y_ps = [psum.tile([P, O], F32, name=f"y_ps{h}", tag=f"narrow{h}") for h in range(2)]
+        y_sb = [keep.tile([P, O], F32, name=f"y_sb{h}") for h in range(2)]
+        for h in range(2):
+            cols = slice(h * P, (h + 1) * P)
+            nc.tensor.matmul_mx(
+                out=y_ps[h][:], lhsT=wb_w[:, cols].bitcast(E2M1), lhsT_scale=wb_s[:, cols],
+                rhs=hid_w[:].bitcast(E4M3), rhs_scale=hid_s[:], start=True, stop=True,
+            )
+        nc.vector.tensor_copy(out=y_sb[0][:], in_=y_ps[0][:])
+        nc.sync.dma_start(out=out[0:P, :], in_=y_sb[0][:])
+        nc.scalar.copy(out=y_sb[1][:], in_=y_ps[1][:])
+        nc.scalar.dma_start(out=out[P : 2 * P, :], in_=y_sb[1][:])

@@ -43,7 +43,6 @@ def tile_list_boardanswer_twow_one_plain_kernel(
     nc = tc.nc
     with ExitStack() as ctx:
         keep = ctx.enter_context(tc.tile_pool(name="keep", bufs=1))
-        ring = ctx.enter_context(tc.tile_pool(name="ring", bufs=4))
         psum = ctx.enter_context(tc.psum_pool(name="psum", bufs=1))
 
         list1 = keep.tile([P, J // 16], U16, name="list1")
@@ -56,7 +55,7 @@ def tile_list_boardanswer_twow_one_plain_kernel(
         xt_s = keep.tile([P, T], U8, name="xt_s", align_bytes=64)
         w_w = keep.tile([P, R], U16, name="w_w", align_bytes=64)
         w_s = keep.tile([P, 4, R], U8, name="w_s", align_bytes=64)
-        w2_w = keep.tile([P, R], U32, name="w2_w", align_bytes=64)
+        w2_w = keep.tile([P, R], U32, name="w2_w", tag="w2_then_a2", align_bytes=64)
         w2_s = keep.tile([P, R], U8, name="w2_s", align_bytes=64)
         wb_w = keep.tile([P, N], U16, name="wb_w", align_bytes=64)
         wb_s = keep.tile([P, N], U8, name="wb_s", align_bytes=64)
@@ -81,14 +80,14 @@ def tile_list_boardanswer_twow_one_plain_kernel(
         )
         load_scale_rows(nc.sync, xt_s, xt_scales, range(4))
         nc.sync.dma_start(list1[:], offs)
-        nc.gpsimd.dma_start(out=sa_t[:], in_=sa.rearrange("(p t) one -> p (t one)", t=PACK))
-        nc.gpsimd.dma_start(out=sb_t[:], in_=sb.rearrange("(p t) one -> p (t one)", t=PACK))
         nc.sync.dma_start(list2[:], offs2)
-        nc.sync.dma_start(out=w2_w[:].bitcast(I32), in_=w2_words[0].rearrange("p n t -> p (n t)").bitcast(I32))
         load_scale_rows(nc.sync, w2_s, w2_scales, range(4))
-        nc.sync.dma_start(list5[:], offs5)
-        nc.sync.dma_start(list4[:], offs4)
+        nc.sync.dma_start(out=w2_w[:].bitcast(I32), in_=w2_words[0].rearrange("p n t -> p (n t)").bitcast(I32))
         nc.sync.dma_start(list3[:], offs3)
+        nc.sync.dma_start(out=sa_t[:], in_=sa.rearrange("(p t) one -> p (t one)", t=PACK))
+        nc.sync.dma_start(list5[:], offs5)
+        nc.sync.dma_start(out=sb_t[:], in_=sb.rearrange("(p t) one -> p (t one)", t=PACK))
+        nc.sync.dma_start(list4[:], offs4)
         nc.sync.dma_start(out=wb_w[:].bitcast(I32), in_=wb_words[0].bitcast(I32))
         load_scale_rows(nc.sync, wb_s, wb_scales, range(4))
 
@@ -103,18 +102,14 @@ def tile_list_boardanswer_twow_one_plain_kernel(
         deal(nc.vector, w_wd[:], w_w[:], 8, slice(0, 4))
         nc.vector.tensor_copy(out=w_s_words[32:36, 0 : 3 * row], in_=w_s_words[0:4, row : 4 * row])
         nc.vector.tensor_copy(out=w_s_words[64:128, 0:row], in_=w_s_words[0:64, 2 * row : 3 * row])
-        deal(nc.gpsimd, w_sd[:], w_s[:, 0, :], 16, slice(0, 2))
-        deal(nc.gpsimd, w_sd[:], w_s[:, 0, :], 16, slice(2, 4))
+        deal(nc.vector, w_sd[:], w_s[:, 0, :], 16, slice(0, 4))
         for h in range(2):
             nc.vector.tensor_copy(x_s[:, h * H : (h + 1) * H], xt_s[:].indirect(list1[:, h * 8 : (h + 1) * 8]))
             nc.vector.tensor_copy(x_w[:, h * H : (h + 1) * H], xt_w[:].indirect(list1[:, h * 8 : (h + 1) * 8]))
-        deal(nc.gpsimd, w2_wd[:], w2_w[:], 4, slice(0, 4))
-        deal(nc.gpsimd, w2_sd[:], w2_s[:], 16, slice(0, 4))
+        deal(nc.vector, w2_sd[:], w2_s[:], 16, slice(0, 4))
+        deal(nc.vector, w2_wd[:], w2_w[:], 4, slice(0, 4))
 
-        early_ps = [psum.tile([P, H], F32, name=f"early_ps{e}", tag=f"narrow{e}") for e in range(2)]
-        late_ps = [psum.tile([P, H], F32, name=f"late_ps{e}") for e in range(2)]
-        whole_ps = [psum.tile([P, J], F32, name=f"whole_ps{e}") for e in range(2)]
-        b_ps = [psum.tile([P, 2, J], F32, name=f"b_ps{h}") for h in range(2)]
+        early_ps = [psum.tile([P, H], F32, name=f"early_ps{e}", tag=f"bank{e}") for e in range(2)]
 
         def first_product(dst, t, lo, hi):
             cols = slice(t * P, (t + 1) * P)
@@ -125,23 +120,14 @@ def tile_list_boardanswer_twow_one_plain_kernel(
 
         first_product(early_ps[0][:], 0, 0, H)
         first_product(early_ps[1][:], 1, 0, H)
-        first_product(late_ps[0][:], 0, H, J)
-        first_product(late_ps[1][:], 1, H, J)
-        first_product(whole_ps[0][:], 3, 0, J)
-        first_product(whole_ps[1][:], 2, 0, J)
-        for t in range(PACK):
-            cols = slice(t * P, (t + 1) * P)
-            nc.tensor.matmul_mx(
-                out=b_ps[t // 2][:, t % 2, :], lhsT=w2_wd[:, cols].bitcast(E4M3), lhsT_scale=w2_sd[:, cols],
-                rhs=x_w[:].bitcast(E5M2), rhs_scale=x_s[:], start=True, stop=True,
-            )
 
+        SPLIT = 192
         early_sb = [keep.tile([P, H], F32, name=f"early_sb{e}") for e in range(2)]
-        late_sb = [keep.tile([P, H + J], F32, name=f"late_sb{e}") for e in range(2)]
-        picked = {}
+        a0_sb = keep.tile([P, H], F32, name="a0_sb")
+        a3_sb = keep.tile([P, SPLIT], F32, name="a3_sb")
+        picked = [keep.tile([P, J], F32, name=f"picked{t}") for t in range(PACK)]
         rb = [keep.tile([P, J], F32, name=f"rb{t}") for t in range(PACK)]
         other = [keep.tile([P, O], F32, name=f"other{t}") for t in range(PACK)]
-        own = [keep.tile([P, O], F32, name=f"own{t}") for t in range(PACK)]
         diff = keep.tile([P, PACK, O], F32, name="diff")
 
         def put_scalar(t, lo, hi, values):
@@ -151,73 +137,70 @@ def tile_list_boardanswer_twow_one_plain_kernel(
             nc.vector.tensor_copy(boards[t][:].indirect(list2[:, lo // 16 : hi // 16]), values)
 
         def pick_board(t):
-            picked[t] = ring.tile([P, J], F32, name="picked")
             nc.scalar.activation(
                 out=picked[t][:], in_=boards[t][:].indirect(list3[:]), func=ACT.Copy, scale=sa_t[:, t : t + 1]
             )
 
         def larger(t):
-            nc.vector.tensor_tensor(out=rb[t][:], in0=picked[t][:], in1=b_ps[t // 2][:, t % 2, :], op=ALU.max)
+            nc.vector.tensor_tensor(out=rb[t][:], in0=picked[t][:], in1=b_of[t], op=ALU.max)
 
         def pick_other(t):
             nc.scalar.activation(
                 out=other[t][:], in_=rb[t][:].indirect(list5[:]), func=ACT.Copy, scale=sb_t[:, t : t + 1]
             )
 
-        def pick_own(t):
-            nc.vector.tensor_copy(own[t][:], rb[t][:].indirect(list4[:]))
-
-        def subtract(engine, t):
-            engine.tensor_tensor(out=diff[:, t, :], in0=own[t][:], in1=other[t][:], op=ALU.subtract)
+        def pick_and_subtract(t):
+            nc.vector.tensor_tensor(out=diff[:, t, :], in0=rb[t][:].indirect(list4[:]), in1=other[t][:], op=ALU.subtract)
 
         hid = keep.tile([P, O, PACK], BF16, name="hid", align_bytes=64)
 
-        by_place = diff[:].rearrange("p t o -> p o t")
+        def magnitude(ts):
+            nc.scalar.activation(out=hid[:, :, ts], in_=diff[:].rearrange("p t o -> p o t")[:, :, ts], func=ACT.Abs)
 
-        def magnitude_scalar(places, ts):
-            nc.scalar.activation(out=hid[:, places, ts], in_=by_place[:, places, ts], func=ACT.Abs)
-
-        SPLIT = 128
         nc.scalar.activation(out=early_sb[0][:], in_=early_ps[0][:], func=ACT.Copy)
         nc.vector.tensor_copy(out=early_sb[1][:], in_=early_ps[1][:])
         put_scalar(0, 0, H, early_sb[0][:])
         put_vector(1, 0, H, early_sb[1][:])
-        for cols, banks in ((slice(0, H), late_ps), (slice(H, H + J), whole_ps)):
-            nc.scalar.activation(out=late_sb[0][:, cols], in_=banks[0][:], func=ACT.Copy)
-            nc.vector.tensor_copy(out=late_sb[1][:, cols], in_=banks[1][:])
-        put_scalar(0, H, J, late_sb[0][:, 0:H])
-        put_vector(1, H, J, late_sb[1][:, 0:H])
-        put_scalar(3, 0, SPLIT, late_sb[0][:, H : H + SPLIT])
-        put_vector(2, 0, J, late_sb[1][:, H : H + J])
-        put_vector(3, SPLIT, J, late_sb[0][:, H + SPLIT : H + J])
-        pick_board(0)
-        pick_board(1)
-        pick_board(2)
-        larger(0)
-        larger(1)
-        pick_other(0)
-        pick_own(0)
-        subtract(nc.gpsimd, 0)
-        pick_board(3)
-        larger(2)
-        pick_other(1)
-        pick_own(1)
-        subtract(nc.gpsimd, 1)
-        larger(3)
-        pick_other(2)
-        pick_own(2)
-        pick_other(3)
-        pick_own(3)
-        subtract(nc.vector, 2)
-        subtract(nc.vector, 3)
-        magnitude_scalar(slice(0, O), slice(0, 2))
-        magnitude_scalar(slice(0, O), slice(2, 4))
+        late_ps = [psum.tile([P, H + J], F32, name=f"late_ps{e}", tag=f"bank{e}") for e in range(2)]
+        first_product(late_ps[0][:, 0:H], 0, H, J)
+        first_product(late_ps[0][:, H : H + J], 3, 0, J)
+        first_product(late_ps[1][:, 0:H], 1, H, J)
+        first_product(late_ps[1][:, H : H + J], 2, 0, J)
+        nc.scalar.activation(out=a0_sb[:], in_=late_ps[0][:, 0:H], func=ACT.Copy)
+        nc.scalar.activation(out=a3_sb[:], in_=late_ps[0][:, H : H + SPLIT], func=ACT.Copy)
+        put_scalar(0, H, J, a0_sb[:])
+        put_scalar(3, 0, SPLIT, a3_sb[:])
+        rest_sb = keep.tile([P, H + 2 * J - SPLIT], F32, name="rest_sb", tag="w2_then_a2", align_bytes=64)
+        nc.vector.tensor_copy(out=rest_sb[:, 0 : H + J], in_=late_ps[1][:])
+        nc.vector.tensor_copy(out=rest_sb[:, H + J :], in_=late_ps[0][:, H + SPLIT : H + J])
+        put_vector(1, H, J, rest_sb[:, 0:H])
+        put_vector(2, 0, J, rest_sb[:, H : H + J])
+        put_vector(3, SPLIT, J, rest_sb[:, H + J :])
+        order = (0, 1, 2, 3)
+        b_ps = [psum.tile([P, 2, J], F32, name=f"b_ps{h}", tag=f"bank{1 - h}") for h in range(2)]
+        b_of = {t: b_ps[n // 2][:, n % 2, :] for n, t in enumerate(order)}
+        for t in order:
+            cols = slice(t * P, (t + 1) * P)
+            nc.tensor.matmul_mx(
+                out=b_of[t], lhsT=w2_wd[:, cols].bitcast(E4M3), lhsT_scale=w2_sd[:, cols],
+                rhs=x_w[:].bitcast(E5M2), rhs_scale=x_s[:], start=True, stop=True,
+            )
+        for t in order:
+            pick_board(t)
+        for t in order:
+            larger(t)
+        for t in order:
+            pick_other(t)
+        for t in order:
+            pick_and_subtract(t)
+        magnitude(slice(0, 2))
+        magnitude(slice(2, 4))
 
         hid_w = keep.tile([P, O], U32, name="hid_w", align_bytes=64)
         hid_s = keep.tile([P, O], U8, name="hid_s", align_bytes=64)
         nc.vector.quantize_mx(out=hid_w[:].bitcast(E4M3), scales=hid_s[:], in_=hid[:].rearrange("p o t -> p (o t)"))
 
-        y_ps = [psum.tile([P, O], F32, name=f"y_ps{h}", tag=f"narrow{h}") for h in range(2)]
+        y_ps = [psum.tile([P, O], F32, name=f"y_ps{h}") for h in range(2)]
         y_sb = [keep.tile([P, O], F32, name=f"y_sb{h}") for h in range(2)]
         for h in range(2):
             cols = slice(h * P, (h + 1) * P)

@@ -54,8 +54,9 @@ def tile_list_boardanswer_twow_one_plain_kernel(
         xt_w = keep.tile([P, T], U32, name="xt_w", align_bytes=64)
         xt_s = keep.tile([P, T], U8, name="xt_s", align_bytes=64)
         w_w = keep.tile([P, R], U16, name="w_w", align_bytes=64)
-        w_s = keep.tile([P, 4, R], U8, name="w_s", align_bytes=64)
-        w2_w = keep.tile([P, R], U32, name="w2_w", tag="w2_then_a2", align_bytes=64)
+        w_rows = keep.tile([4, 4, R // 4], I32, name="w_rows")
+        w_s = keep.tile([P, 2, R], U8, name="w_s", align_bytes=64)
+        w2_w = keep.tile([P, R], U32, name="w2_w", align_bytes=64)
         w2_s = keep.tile([P, R], U8, name="w2_s", align_bytes=64)
         wb_w = keep.tile([P, N], U16, name="wb_w", align_bytes=64)
         wb_s = keep.tile([P, N], U8, name="wb_s", align_bytes=64)
@@ -65,24 +66,22 @@ def tile_list_boardanswer_twow_one_plain_kernel(
 
         w_s_words = w_s[:].rearrange("p q c -> p (q c)").bitcast(I32)
         row = R // 4
-        nc.vector.memset(w_s_words.rearrange("p (a b c) -> p a b c", a=2, b=2)[:, :, 0, :], 0)
         nc.vector.memset(xt_s[:].bitcast(I32), 0)
+        nc.vector.memset(w_s_words, 0)
         for plane in (w2_s, wb_s):
-            nc.vector.memset(plane[:].bitcast(I32), 0)
+            nc.gpsimd.memset(plane[:].bitcast(I32), 0)
         for t in range(PACK):
-            nc.vector.memset(boards[t][:], 0.0)
+            (nc.vector if t < 2 else nc.gpsimd).memset(boards[t][:], 0.0)
 
-        nc.sync.dma_start(out=w_w[:].bitcast(I32), in_=w_words[0].bitcast(I32))
-        nc.scalar.dma_start(out=xt_w[:].bitcast(I32), in_=xt_words[0].rearrange("p n t -> p (n t)").bitcast(I32))
-        nc.sync.dma_start(
-            out=w_s_words[0:4, :].rearrange("r (q c) -> r q c", q=4),
-            in_=w_scales[0].bitcast(I32).rearrange("(q r) c -> r q c", r=4),
-        )
-        load_scale_rows(nc.sync, xt_s, xt_scales, range(4))
+        nc.sync.dma_start(out=w_rows[:], in_=w_scales[0].bitcast(I32).rearrange("(q r) c -> r q c", r=4))
+        nc.scalar.dma_start(out=w_w[:].bitcast(I32), in_=w_words[0].bitcast(I32))
         nc.sync.dma_start(list1[:], offs)
+        load_scale_rows(nc.scalar, xt_s, xt_scales, (0, 2))
+        load_scale_rows(nc.sync, xt_s, xt_scales, (1, 3))
+        nc.scalar.dma_start(out=xt_w[:].bitcast(I32), in_=xt_words[0].rearrange("p n t -> p (n t)").bitcast(I32))
         nc.sync.dma_start(list2[:], offs2)
-        load_scale_rows(nc.sync, w2_s, w2_scales, range(4))
         nc.sync.dma_start(out=w2_w[:].bitcast(I32), in_=w2_words[0].rearrange("p n t -> p (n t)").bitcast(I32))
+        load_scale_rows(nc.sync, w2_s, w2_scales, range(4))
         nc.sync.dma_start(list3[:], offs3)
         nc.sync.dma_start(out=sa_t[:], in_=sa.rearrange("(p t) one -> p (t one)", t=PACK))
         nc.sync.dma_start(list5[:], offs5)
@@ -99,15 +98,23 @@ def tile_list_boardanswer_twow_one_plain_kernel(
         w2_sd = keep.tile([P, R], U8, name="w2_sd", align_bytes=64)
 
         H = J // 2
-        deal(nc.vector, w_wd[:], w_w[:], 8, slice(0, 4))
-        nc.vector.tensor_copy(out=w_s_words[32:36, 0 : 3 * row], in_=w_s_words[0:4, row : 4 * row])
-        nc.vector.tensor_copy(out=w_s_words[64:128, 0:row], in_=w_s_words[0:64, 2 * row : 3 * row])
-        deal(nc.vector, w_sd[:], w_s[:, 0, :], 16, slice(0, 4))
+        nc.scalar.copy(
+            out=w_wd[:].rearrange("p (t c i) -> p c t i", t=PACK, i=8),
+            in_=w_w[:].rearrange("p (c i t) -> p c t i", t=PACK, i=8),
+        )
+        by_half = w_rows[:].rearrange("r (a b) c -> r b a c", b=2)
+        for b in range(2):
+            nc.vector.tensor_copy(
+                out=w_s_words[32 * b : 32 * b + 4, :].rearrange("r (a c) -> r a c", a=2), in_=by_half[:, b]
+            )
+        nc.vector.tensor_copy(out=w_s_words[64:128, 0:row], in_=w_s_words[0:64, row : 2 * row])
+        deal(nc.gpsimd, w_sd[:], w_s[:, 0, :], 16, slice(0, 2))
+        deal(nc.gpsimd, w_sd[:], w_s[:, 0, :], 16, slice(2, 4))
+        nc.vector.tensor_copy(x_s[:], xt_s[:].indirect(list1[:]))
         for h in range(2):
-            nc.vector.tensor_copy(x_s[:, h * H : (h + 1) * H], xt_s[:].indirect(list1[:, h * 8 : (h + 1) * 8]))
             nc.vector.tensor_copy(x_w[:, h * H : (h + 1) * H], xt_w[:].indirect(list1[:, h * 8 : (h + 1) * 8]))
-        deal(nc.vector, w2_sd[:], w2_s[:], 16, slice(0, 4))
-        deal(nc.vector, w2_wd[:], w2_w[:], 4, slice(0, 4))
+        deal(nc.gpsimd, w2_wd[:], w2_w[:], 4, slice(0, 4))
+        deal(nc.gpsimd, w2_sd[:], w2_s[:], 16, slice(0, 4))
 
         early_ps = [psum.tile([P, H], F32, name=f"early_ps{e}", tag=f"bank{e}") for e in range(2)]
 
@@ -121,10 +128,8 @@ def tile_list_boardanswer_twow_one_plain_kernel(
         first_product(early_ps[0][:], 0, 0, H)
         first_product(early_ps[1][:], 1, 0, H)
 
-        SPLIT = 192
-        early_sb = [keep.tile([P, H], F32, name=f"early_sb{e}") for e in range(2)]
-        a0_sb = keep.tile([P, H], F32, name="a0_sb")
-        a3_sb = keep.tile([P, SPLIT], F32, name="a3_sb")
+        SPLIT = 160
+        early_sb = [keep.tile([P, H], F32, name=f"early_sb{e}", tag=f"staged{e}") for e in range(2)]
         picked = [keep.tile([P, J], F32, name=f"picked{t}") for t in range(PACK)]
         rb = [keep.tile([P, J], F32, name=f"rb{t}") for t in range(PACK)]
         other = [keep.tile([P, O], F32, name=f"other{t}") for t in range(PACK)]
@@ -154,30 +159,42 @@ def tile_list_boardanswer_twow_one_plain_kernel(
 
         hid = keep.tile([P, O, PACK], BF16, name="hid", align_bytes=64)
 
-        def magnitude(ts):
-            nc.scalar.activation(out=hid[:, :, ts], in_=diff[:].rearrange("p t o -> p o t")[:, :, ts], func=ACT.Abs)
+        by_place = diff[:].rearrange("p t o -> p o t")
+
+        def magnitude_scalar(places, ts):
+            nc.scalar.activation(out=hid[:, places, ts], in_=by_place[:, places, ts], func=ACT.Abs)
+
+        def magnitude_vector(places, ts):
+            nc.vector.scalar_tensor_tensor(
+                out=hid[:, places, ts], in0=by_place[:, places, ts], scalar=-1.0, in1=by_place[:, places, ts],
+                op0=ALU.mult, op1=ALU.max,
+            )
 
         nc.scalar.activation(out=early_sb[0][:], in_=early_ps[0][:], func=ACT.Copy)
         nc.vector.tensor_copy(out=early_sb[1][:], in_=early_ps[1][:])
         put_scalar(0, 0, H, early_sb[0][:])
         put_vector(1, 0, H, early_sb[1][:])
-        late_ps = [psum.tile([P, H + J], F32, name=f"late_ps{e}", tag=f"bank{e}") for e in range(2)]
-        first_product(late_ps[0][:, 0:H], 0, H, J)
-        first_product(late_ps[0][:, H : H + J], 3, 0, J)
-        first_product(late_ps[1][:, 0:H], 1, H, J)
-        first_product(late_ps[1][:, H : H + J], 2, 0, J)
-        nc.scalar.activation(out=a0_sb[:], in_=late_ps[0][:, 0:H], func=ACT.Copy)
-        nc.scalar.activation(out=a3_sb[:], in_=late_ps[0][:, H : H + SPLIT], func=ACT.Copy)
-        put_scalar(0, H, J, a0_sb[:])
-        put_scalar(3, 0, SPLIT, a3_sb[:])
-        rest_sb = keep.tile([P, H + 2 * J - SPLIT], F32, name="rest_sb", tag="w2_then_a2", align_bytes=64)
-        nc.vector.tensor_copy(out=rest_sb[:, 0 : H + J], in_=late_ps[1][:])
-        nc.vector.tensor_copy(out=rest_sb[:, H + J :], in_=late_ps[0][:, H + SPLIT : H + J])
-        put_vector(1, H, J, rest_sb[:, 0:H])
-        put_vector(2, 0, J, rest_sb[:, H : H + J])
-        put_vector(3, SPLIT, J, rest_sb[:, H + J :])
+        late_ps = [psum.tile([P, H], F32, name=f"late_ps{e}") for e in range(2)]
+        a3_ps = psum.tile([P, J], F32, name="a3_ps")
+        a2_ps = psum.tile([P, J], F32, name="a2_ps")
+        first_product(late_ps[0][:], 0, H, J)
+        first_product(late_ps[1][:], 1, H, J)
+        first_product(a3_ps[:], 3, 0, J)
+        first_product(a2_ps[:], 2, 0, J)
+        s_sb = keep.tile([P, H + SPLIT], F32, name="s_sb", tag="staged0")
+        nc.scalar.activation(out=s_sb[:, 0:H], in_=late_ps[0][:], func=ACT.Copy)
+        nc.scalar.activation(out=s_sb[:, H:], in_=a3_ps[:, 0:SPLIT], func=ACT.Copy)
+        put_scalar(0, H, J, s_sb[:, 0:H])
+        put_scalar(3, 0, SPLIT, s_sb[:, H:])
+        v_sb = keep.tile([P, H + 2 * J - SPLIT], F32, name="v_sb", tag="staged1")
+        nc.vector.tensor_copy(out=v_sb[:, 0:H], in_=late_ps[1][:])
+        nc.vector.tensor_copy(out=v_sb[:, H : H + J], in_=a2_ps[:])
+        nc.vector.tensor_copy(out=v_sb[:, H + J :], in_=a3_ps[:, SPLIT:J])
+        put_vector(1, H, J, v_sb[:, 0:H])
+        put_vector(2, 0, J, v_sb[:, H : H + J])
+        put_vector(3, SPLIT, J, v_sb[:, H + J :])
         order = (0, 1, 2, 3)
-        b_ps = [psum.tile([P, 2, J], F32, name=f"b_ps{h}", tag=f"bank{1 - h}") for h in range(2)]
+        b_ps = [psum.tile([P, 2, J], F32, name=f"b_ps{h}") for h in range(2)]
         b_of = {t: b_ps[n // 2][:, n % 2, :] for n, t in enumerate(order)}
         for t in order:
             cols = slice(t * P, (t + 1) * P)
@@ -193,14 +210,15 @@ def tile_list_boardanswer_twow_one_plain_kernel(
             pick_other(t)
         for t in order:
             pick_and_subtract(t)
-        magnitude(slice(0, 2))
-        magnitude(slice(2, 4))
+        magnitude_scalar(slice(0, O), slice(0, 2))
+        magnitude_scalar(slice(0, O // 2), slice(2, 4))
+        magnitude_vector(slice(O // 2, O), slice(2, 4))
 
         hid_w = keep.tile([P, O], U32, name="hid_w", align_bytes=64)
         hid_s = keep.tile([P, O], U8, name="hid_s", align_bytes=64)
         nc.vector.quantize_mx(out=hid_w[:].bitcast(E4M3), scales=hid_s[:], in_=hid[:].rearrange("p o t -> p (o t)"))
 
-        y_ps = [psum.tile([P, O], F32, name=f"y_ps{h}") for h in range(2)]
+        y_ps = [psum.tile([P, O], F32, name=f"y_ps{h}", tag=f"bank{h}") for h in range(2)]
         y_sb = [keep.tile([P, O], F32, name=f"y_sb{h}") for h in range(2)]
         for h in range(2):
             cols = slice(h * P, (h + 1) * P)

@@ -69,16 +69,15 @@ def tile_list_boardanswer_twow_one_plain_kernel(
         nc.vector.memset(xt_s[:].bitcast(I32), 0)
         nc.vector.memset(w_s_words, 0)
         for plane in (w2_s, wb_s):
-            nc.gpsimd.memset(plane[:].bitcast(I32), 0)
+            nc.vector.memset(plane[:].bitcast(I32), 0)
         for t in range(PACK):
-            (nc.vector if t < 2 else nc.gpsimd).memset(boards[t][:], 0.0)
+            nc.vector.memset(boards[t][:], 0.0)
 
         nc.sync.dma_start(out=w_rows[:], in_=w_scales[0].bitcast(I32).rearrange("(q r) c -> r q c", r=4))
-        nc.scalar.dma_start(out=w_w[:].bitcast(I32), in_=w_words[0].bitcast(I32))
-        nc.sync.dma_start(list1[:], offs)
-        load_scale_rows(nc.scalar, xt_s, xt_scales, (0, 2))
-        load_scale_rows(nc.sync, xt_s, xt_scales, (1, 3))
         nc.scalar.dma_start(out=xt_w[:].bitcast(I32), in_=xt_words[0].rearrange("p n t -> p (n t)").bitcast(I32))
+        nc.sync.dma_start(out=w_w[:].bitcast(I32), in_=w_words[0].bitcast(I32))
+        load_scale_rows(nc.sync, xt_s, xt_scales, range(4))
+        nc.sync.dma_start(list1[:], offs)
         nc.sync.dma_start(list2[:], offs2)
         nc.sync.dma_start(out=w2_w[:].bitcast(I32), in_=w2_words[0].rearrange("p n t -> p (n t)").bitcast(I32))
         load_scale_rows(nc.sync, w2_s, w2_scales, range(4))
@@ -110,8 +109,8 @@ def tile_list_boardanswer_twow_one_plain_kernel(
         nc.vector.tensor_copy(out=w_s_words[64:128, 0:row], in_=w_s_words[0:64, row : 2 * row])
         deal(nc.gpsimd, w_sd[:], w_s[:, 0, :], 16, slice(0, 2))
         deal(nc.gpsimd, w_sd[:], w_s[:, 0, :], 16, slice(2, 4))
-        nc.vector.tensor_copy(x_s[:], xt_s[:].indirect(list1[:]))
         for h in range(2):
+            nc.vector.tensor_copy(x_s[:, h * H : (h + 1) * H], xt_s[:].indirect(list1[:, h * 8 : (h + 1) * 8]))
             nc.vector.tensor_copy(x_w[:, h * H : (h + 1) * H], xt_w[:].indirect(list1[:, h * 8 : (h + 1) * 8]))
         deal(nc.gpsimd, w2_wd[:], w2_w[:], 4, slice(0, 4))
         deal(nc.gpsimd, w2_sd[:], w2_s[:], 16, slice(0, 4))

@@ -19,21 +19,32 @@ ACT = mybir.ActivationFunctionType
 
 P = 128
 PACK = 4
+QUADRANTS = 4
+PER_COLUMN = 16
+LINE = 16
+HALF = J // 2
+ROW_WORDS = R // 4
+SCALAR_SHARE = 160
 
 
-def load_scale_rows(queue, plane, scales, quadrants):
-    for q in quadrants:
-        queue.dma_start(
+def load_scale_rows(nc, plane, scales):
+    for q in range(QUADRANTS):
+        nc.sync.dma_start(
             out=plane[32 * q : 32 * q + 4, :].bitcast(I32),
             in_=scales[0, 4 * q : 4 * q + 4, :].bitcast(I32),
         )
 
 
-def deal(engine, dealt, loaded, line, ts):
-    engine.tensor_copy(
-        out=dealt.rearrange("p (t c i) -> p c t i", t=PACK, i=line)[:, :, ts, :],
-        in_=loaded.rearrange("p (c i t) -> p c t i", t=PACK, i=line)[:, :, ts, :],
+def deal(copy, dealt, loaded, element_bytes, slices):
+    per_line = LINE // element_bytes
+    copy(
+        out=dealt.rearrange("p (t c i) -> p c t i", t=PACK, i=per_line)[:, :, slices, :],
+        in_=loaded.rearrange("p (c i t) -> p c t i", t=PACK, i=per_line)[:, :, slices, :],
     )
+
+
+def entries(list_tile, lo, hi):
+    return list_tile[:, lo // PER_COLUMN : hi // PER_COLUMN]
 
 
 def tile_list_boardanswer_twow_one_plain_kernel(
@@ -45,16 +56,16 @@ def tile_list_boardanswer_twow_one_plain_kernel(
         keep = ctx.enter_context(tc.tile_pool(name="keep", bufs=1))
         psum = ctx.enter_context(tc.psum_pool(name="psum", bufs=1))
 
-        list1 = keep.tile([P, J // 16], U16, name="list1")
-        list2 = keep.tile([P, J // 16], U16, name="list2")
-        list3 = keep.tile([P, J // 16], U16, name="list3")
-        list4 = keep.tile([P, O // 16], U16, name="list4")
-        list5 = keep.tile([P, O // 16], U16, name="list5")
+        list1 = keep.tile([P, J // PER_COLUMN], U16, name="list1")
+        list2 = keep.tile([P, J // PER_COLUMN], U16, name="list2")
+        list3 = keep.tile([P, J // PER_COLUMN], U16, name="list3")
+        list4 = keep.tile([P, O // PER_COLUMN], U16, name="list4")
+        list5 = keep.tile([P, O // PER_COLUMN], U16, name="list5")
 
         xt_w = keep.tile([P, T], U32, name="xt_w", align_bytes=64)
         xt_s = keep.tile([P, T], U8, name="xt_s", align_bytes=64)
         w_w = keep.tile([P, R], U16, name="w_w", align_bytes=64)
-        w_rows = keep.tile([4, 4, R // 4], I32, name="w_rows")
+        w_rows = keep.tile([4, QUADRANTS, ROW_WORDS], I32, name="w_rows")
         w_s = keep.tile([P, 2, R], U8, name="w_s", align_bytes=64)
         w2_w = keep.tile([P, R], U32, name="w2_w", align_bytes=64)
         w2_s = keep.tile([P, R], U8, name="w2_s", align_bytes=64)
@@ -65,7 +76,6 @@ def tile_list_boardanswer_twow_one_plain_kernel(
         boards = [keep.tile([P, C], F32, name=f"board{t}") for t in range(PACK)]
 
         w_s_words = w_s[:].rearrange("p q c -> p (q c)").bitcast(I32)
-        row = R // 4
         nc.vector.memset(xt_s[:].bitcast(I32), 0)
         nc.vector.memset(w_s_words, 0)
         for plane in (w2_s, wb_s):
@@ -75,19 +85,19 @@ def tile_list_boardanswer_twow_one_plain_kernel(
 
         nc.sync.dma_start(out=w_rows[:], in_=w_scales[0].bitcast(I32).rearrange("(q r) c -> r q c", r=4))
         nc.scalar.dma_start(out=xt_w[:].bitcast(I32), in_=xt_words[0].rearrange("p n t -> p (n t)").bitcast(I32))
-        nc.sync.dma_start(out=w_w[:].bitcast(I32), in_=w_words[0].bitcast(I32))
-        load_scale_rows(nc.sync, xt_s, xt_scales, range(4))
+        load_scale_rows(nc, xt_s, xt_scales)
         nc.sync.dma_start(list1[:], offs)
+        nc.sync.dma_start(out=w_w[:].bitcast(I32), in_=w_words[0].bitcast(I32))
         nc.sync.dma_start(list2[:], offs2)
         nc.sync.dma_start(out=w2_w[:].bitcast(I32), in_=w2_words[0].rearrange("p n t -> p (n t)").bitcast(I32))
-        load_scale_rows(nc.sync, w2_s, w2_scales, range(4))
+        load_scale_rows(nc, w2_s, w2_scales)
         nc.sync.dma_start(list3[:], offs3)
         nc.sync.dma_start(out=sa_t[:], in_=sa.rearrange("(p t) one -> p (t one)", t=PACK))
         nc.sync.dma_start(list5[:], offs5)
         nc.sync.dma_start(out=sb_t[:], in_=sb.rearrange("(p t) one -> p (t one)", t=PACK))
         nc.sync.dma_start(list4[:], offs4)
         nc.sync.dma_start(out=wb_w[:].bitcast(I32), in_=wb_words[0].bitcast(I32))
-        load_scale_rows(nc.sync, wb_s, wb_scales, range(4))
+        load_scale_rows(nc, wb_s, wb_scales)
 
         x_w = keep.tile([P, J], U32, name="x_w", align_bytes=64)
         x_s = keep.tile([P, J], U8, name="x_s", align_bytes=64)
@@ -96,26 +106,23 @@ def tile_list_boardanswer_twow_one_plain_kernel(
         w2_wd = keep.tile([P, R], U32, name="w2_wd", align_bytes=64)
         w2_sd = keep.tile([P, R], U8, name="w2_sd", align_bytes=64)
 
-        H = J // 2
-        nc.scalar.copy(
-            out=w_wd[:].rearrange("p (t c i) -> p c t i", t=PACK, i=8),
-            in_=w_w[:].rearrange("p (c i t) -> p c t i", t=PACK, i=8),
-        )
-        by_half = w_rows[:].rearrange("r (a b) c -> r b a c", b=2)
+        first_pair, second_pair, all_slices = slice(0, 2), slice(2, PACK), slice(0, PACK)
+        for pair in (first_pair, second_pair):
+            deal(nc.scalar.copy, w_wd[:], w_w[:], 2, pair)
+        by_parity = w_rows[:].rearrange("r (a b) c -> r b a c", b=2)
         for b in range(2):
             nc.vector.tensor_copy(
-                out=w_s_words[32 * b : 32 * b + 4, :].rearrange("r (a c) -> r a c", a=2), in_=by_half[:, b]
+                out=w_s_words[32 * b : 32 * b + 4, :].rearrange("r (a c) -> r a c", a=2), in_=by_parity[:, b]
             )
-        nc.vector.tensor_copy(out=w_s_words[64:128, 0:row], in_=w_s_words[0:64, row : 2 * row])
-        deal(nc.gpsimd, w_sd[:], w_s[:, 0, :], 16, slice(0, 2))
-        deal(nc.gpsimd, w_sd[:], w_s[:, 0, :], 16, slice(2, 4))
-        for h in range(2):
-            nc.vector.tensor_copy(x_s[:, h * H : (h + 1) * H], xt_s[:].indirect(list1[:, h * 8 : (h + 1) * 8]))
-            nc.vector.tensor_copy(x_w[:, h * H : (h + 1) * H], xt_w[:].indirect(list1[:, h * 8 : (h + 1) * 8]))
-        deal(nc.gpsimd, w2_wd[:], w2_w[:], 4, slice(0, 4))
-        deal(nc.gpsimd, w2_sd[:], w2_s[:], 16, slice(0, 4))
-
-        early_ps = [psum.tile([P, H], F32, name=f"early_ps{e}", tag=f"bank{e}") for e in range(2)]
+        nc.vector.tensor_copy(out=w_s_words[64:128, 0:ROW_WORDS], in_=w_s_words[0:64, ROW_WORDS : 2 * ROW_WORDS])
+        for pair in (first_pair, second_pair):
+            deal(nc.gpsimd.tensor_copy, w_sd[:], w_s[:, 0, :], 1, pair)
+        for lo in (0, HALF):
+            slots = entries(list1, lo, lo + HALF)
+            nc.vector.tensor_copy(x_s[:, lo : lo + HALF], xt_s[:].indirect(slots))
+            nc.vector.tensor_copy(x_w[:, lo : lo + HALF], xt_w[:].indirect(slots))
+        deal(nc.gpsimd.tensor_copy, w2_wd[:], w2_w[:], 4, all_slices)
+        deal(nc.gpsimd.tensor_copy, w2_sd[:], w2_s[:], 1, all_slices)
 
         def first_product(dst, t, lo, hi):
             cols = slice(t * P, (t + 1) * P)
@@ -124,94 +131,78 @@ def tile_list_boardanswer_twow_one_plain_kernel(
                 rhs=x_w[:, lo:hi].bitcast(E5M2), rhs_scale=x_s[:, lo:hi], start=True, stop=True,
             )
 
-        first_product(early_ps[0][:], 0, 0, H)
-        first_product(early_ps[1][:], 1, 0, H)
+        early_ps = [psum.tile([P, HALF], F32, name=f"early_ps{t}", tag=f"bank{t}") for t in range(2)]
+        for t in range(2):
+            first_product(early_ps[t][:], t, 0, HALF)
 
-        SPLIT = 160
-        early_sb = [keep.tile([P, H], F32, name=f"early_sb{e}", tag=f"staged{e}") for e in range(2)]
+        early_sb = [keep.tile([P, HALF], F32, name=f"early_sb{t}", tag=f"staged{t}") for t in range(2)]
         picked = [keep.tile([P, J], F32, name=f"picked{t}") for t in range(PACK)]
         rb = [keep.tile([P, J], F32, name=f"rb{t}") for t in range(PACK)]
         other = [keep.tile([P, O], F32, name=f"other{t}") for t in range(PACK)]
         diff = keep.tile([P, PACK, O], F32, name="diff")
-
-        def put_scalar(t, lo, hi, values):
-            nc.scalar.activation(out=boards[t][:].indirect(list2[:, lo // 16 : hi // 16]), in_=values, func=ACT.Copy)
-
-        def put_vector(t, lo, hi, values):
-            nc.vector.tensor_copy(boards[t][:].indirect(list2[:, lo // 16 : hi // 16]), values)
-
-        def pick_board(t):
-            nc.scalar.activation(
-                out=picked[t][:], in_=boards[t][:].indirect(list3[:]), func=ACT.Copy, scale=sa_t[:, t : t + 1]
-            )
-
-        def larger(t):
-            nc.vector.tensor_tensor(out=rb[t][:], in0=picked[t][:], in1=b_of[t], op=ALU.max)
-
-        def pick_other(t):
-            nc.scalar.activation(
-                out=other[t][:], in_=rb[t][:].indirect(list5[:]), func=ACT.Copy, scale=sb_t[:, t : t + 1]
-            )
-
-        def pick_and_subtract(t):
-            nc.vector.tensor_tensor(out=diff[:, t, :], in0=rb[t][:].indirect(list4[:]), in1=other[t][:], op=ALU.subtract)
-
         hid = keep.tile([P, O, PACK], BF16, name="hid", align_bytes=64)
 
-        by_place = diff[:].rearrange("p t o -> p o t")
+        def put_scalar(t, lo, hi, values):
+            nc.scalar.activation(out=boards[t][:].indirect(entries(list2, lo, hi)), in_=values, func=ACT.Copy)
 
-        def magnitude_scalar(places, ts):
-            nc.scalar.activation(out=hid[:, places, ts], in_=by_place[:, places, ts], func=ACT.Abs)
-
-        def magnitude_vector(places, ts):
-            nc.vector.scalar_tensor_tensor(
-                out=hid[:, places, ts], in0=by_place[:, places, ts], scalar=-1.0, in1=by_place[:, places, ts],
-                op0=ALU.mult, op1=ALU.max,
-            )
+        def put_vector(t, lo, hi, values):
+            nc.vector.tensor_copy(boards[t][:].indirect(entries(list2, lo, hi)), values)
 
         nc.scalar.activation(out=early_sb[0][:], in_=early_ps[0][:], func=ACT.Copy)
         nc.vector.tensor_copy(out=early_sb[1][:], in_=early_ps[1][:])
-        put_scalar(0, 0, H, early_sb[0][:])
-        put_vector(1, 0, H, early_sb[1][:])
-        late_ps = [psum.tile([P, H], F32, name=f"late_ps{e}") for e in range(2)]
+        put_scalar(0, 0, HALF, early_sb[0][:])
+        put_vector(1, 0, HALF, early_sb[1][:])
+
+        late_ps = [psum.tile([P, HALF], F32, name=f"late_ps{t}") for t in range(2)]
         a3_ps = psum.tile([P, J], F32, name="a3_ps")
         a2_ps = psum.tile([P, J], F32, name="a2_ps")
-        first_product(late_ps[0][:], 0, H, J)
-        first_product(late_ps[1][:], 1, H, J)
+        for t in range(2):
+            first_product(late_ps[t][:], t, HALF, J)
         first_product(a3_ps[:], 3, 0, J)
         first_product(a2_ps[:], 2, 0, J)
-        s_sb = keep.tile([P, H + SPLIT], F32, name="s_sb", tag="staged0")
-        nc.scalar.activation(out=s_sb[:, 0:H], in_=late_ps[0][:], func=ACT.Copy)
-        nc.scalar.activation(out=s_sb[:, H:], in_=a3_ps[:, 0:SPLIT], func=ACT.Copy)
-        put_scalar(0, H, J, s_sb[:, 0:H])
-        put_scalar(3, 0, SPLIT, s_sb[:, H:])
-        v_sb = keep.tile([P, H + 2 * J - SPLIT], F32, name="v_sb", tag="staged1")
-        nc.vector.tensor_copy(out=v_sb[:, 0:H], in_=late_ps[1][:])
-        nc.vector.tensor_copy(out=v_sb[:, H : H + J], in_=a2_ps[:])
-        nc.vector.tensor_copy(out=v_sb[:, H + J :], in_=a3_ps[:, SPLIT:J])
-        put_vector(1, H, J, v_sb[:, 0:H])
-        put_vector(2, 0, J, v_sb[:, H : H + J])
-        put_vector(3, SPLIT, J, v_sb[:, H + J :])
-        order = (0, 1, 2, 3)
+
+        s_sb = keep.tile([P, HALF + SCALAR_SHARE], F32, name="s_sb", tag="staged0")
+        nc.scalar.activation(out=s_sb[:, 0:HALF], in_=late_ps[0][:], func=ACT.Copy)
+        nc.scalar.activation(out=s_sb[:, HALF:], in_=a3_ps[:, 0:SCALAR_SHARE], func=ACT.Copy)
+        put_scalar(0, HALF, J, s_sb[:, 0:HALF])
+        put_scalar(3, 0, SCALAR_SHARE, s_sb[:, HALF:])
+        v_sb = keep.tile([P, HALF + 2 * J - SCALAR_SHARE], F32, name="v_sb", tag="staged1")
+        nc.vector.tensor_copy(out=v_sb[:, 0:HALF], in_=late_ps[1][:])
+        nc.vector.tensor_copy(out=v_sb[:, HALF : HALF + J], in_=a2_ps[:])
+        nc.vector.tensor_copy(out=v_sb[:, HALF + J :], in_=a3_ps[:, SCALAR_SHARE:J])
+        put_vector(1, HALF, J, v_sb[:, 0:HALF])
+        put_vector(2, 0, J, v_sb[:, HALF : HALF + J])
+        put_vector(3, SCALAR_SHARE, J, v_sb[:, HALF + J :])
+
         b_ps = [psum.tile([P, 2, J], F32, name=f"b_ps{h}") for h in range(2)]
-        b_of = {t: b_ps[n // 2][:, n % 2, :] for n, t in enumerate(order)}
-        for t in order:
+        for t in range(PACK):
             cols = slice(t * P, (t + 1) * P)
             nc.tensor.matmul_mx(
-                out=b_of[t], lhsT=w2_wd[:, cols].bitcast(E4M3), lhsT_scale=w2_sd[:, cols],
+                out=b_ps[t // 2][:, t % 2, :], lhsT=w2_wd[:, cols].bitcast(E4M3), lhsT_scale=w2_sd[:, cols],
                 rhs=x_w[:].bitcast(E5M2), rhs_scale=x_s[:], start=True, stop=True,
             )
-        for t in order:
-            pick_board(t)
-        for t in order:
-            larger(t)
-        for t in order:
-            pick_other(t)
-        for t in order:
-            pick_and_subtract(t)
-        magnitude_scalar(slice(0, O), slice(0, 2))
-        magnitude_scalar(slice(0, O // 2), slice(2, 4))
-        magnitude_vector(slice(O // 2, O), slice(2, 4))
+
+        for t in range(PACK):
+            nc.scalar.activation(
+                out=picked[t][:], in_=boards[t][:].indirect(list3[:]), func=ACT.Copy, scale=sa_t[:, t : t + 1]
+            )
+        for t in range(PACK):
+            nc.vector.tensor_tensor(out=rb[t][:], in0=picked[t][:], in1=b_ps[t // 2][:, t % 2, :], op=ALU.max)
+        for t in range(PACK):
+            nc.scalar.activation(
+                out=other[t][:], in_=rb[t][:].indirect(list5[:]), func=ACT.Copy, scale=sb_t[:, t : t + 1]
+            )
+        for t in range(PACK):
+            nc.vector.tensor_tensor(out=diff[:, t, :], in0=rb[t][:].indirect(list4[:]), in1=other[t][:], op=ALU.subtract)
+
+        by_place = diff[:].rearrange("p t o -> p o t")
+        low, high = slice(0, O // 2), slice(O // 2, O)
+        nc.scalar.activation(out=hid[:, :, first_pair], in_=by_place[:, :, first_pair], func=ACT.Abs)
+        nc.scalar.activation(out=hid[:, low, second_pair], in_=by_place[:, low, second_pair], func=ACT.Abs)
+        nc.vector.scalar_tensor_tensor(
+            out=hid[:, high, second_pair], in0=by_place[:, high, second_pair], scalar=-1.0,
+            in1=by_place[:, high, second_pair], op0=ALU.mult, op1=ALU.max,
+        )
 
         hid_w = keep.tile([P, O], U32, name="hid_w", align_bytes=64)
         hid_s = keep.tile([P, O], U8, name="hid_s", align_bytes=64)

from contextlib import ExitStack

import concourse.mybir as mybir

K, T, J, R, C, O, N = 512, 1024, 256, 512, 512, 128, 256
FLOPS = 2 * K * R * J * 2 + 2 * R * N * O

F32 = mybir.dt.float32
BF16 = mybir.dt.bfloat16
I32 = mybir.dt.int32
U32 = mybir.dt.uint32
U16 = mybir.dt.uint16
U8 = mybir.dt.uint8
E4M3 = mybir.dt.float8_e4m3fn_x4
E5M2 = mybir.dt.float8_e5m2_x4
E2M1 = mybir.dt.float4_e2m1fn_x4
ALU = mybir.AluOpType
ACT = mybir.ActivationFunctionType

P = 128
PACK = 4
QUADRANTS = 4
PER_COLUMN = 16
LINE = 16
HALF = J // 2
ROW_WORDS = R // 4
SCALAR_SHARE = 160


def load_scale_rows(nc, plane, scales):
    for q in range(QUADRANTS):
        nc.sync.dma_start(
            out=plane[32 * q : 32 * q + 4, :].bitcast(I32),
            in_=scales[0, 4 * q : 4 * q + 4, :].bitcast(I32),
        )


def deal(copy, dealt, loaded, element_bytes, slices):
    per_line = LINE // element_bytes
    copy(
        out=dealt.rearrange("p (t c i) -> p c t i", t=PACK, i=per_line)[:, :, slices, :],
        in_=loaded.rearrange("p (c i t) -> p c t i", t=PACK, i=per_line)[:, :, slices, :],
    )


def entries(list_tile, lo, hi):
    return list_tile[:, lo // PER_COLUMN : hi // PER_COLUMN]


def tile_list_boardanswer_twow_one_plain_kernel(
    tc, xt_words, xt_scales, w_words, w_scales, w2_words, w2_scales, sa, sb, wb_words, wb_scales,
    offs, offs2, offs3, offs4, offs5, out,
):
    nc = tc.nc
    with ExitStack() as ctx:
        keep = ctx.enter_context(tc.tile_pool(name="keep", bufs=1))
        psum = ctx.enter_context(tc.psum_pool(name="psum", bufs=1))

        list1 = keep.tile([P, J // PER_COLUMN], U16, name="list1")
        list2 = keep.tile([P, J // PER_COLUMN], U16, name="list2")
        list3 = keep.tile([P, J // PER_COLUMN], U16, name="list3")
        list4 = keep.tile([P, O // PER_COLUMN], U16, name="list4")
        list5 = keep.tile([P, O // PER_COLUMN], U16, name="list5")

        xt_w = keep.tile([P, T], U32, name="xt_w", align_bytes=64)
        xt_s = keep.tile([P, T], U8, name="xt_s", align_bytes=64)
        w_w = keep.tile([P, R], U16, name="w_w", align_bytes=64)
        w_rows = keep.tile([4, QUADRANTS, ROW_WORDS], I32, name="w_rows")
        w_s = keep.tile([P, 2, R], U8, name="w_s", align_bytes=64)
        w2_w = keep.tile([P, R], U32, name="w2_w", align_bytes=64)
        w2_s = keep.tile([P, R], U8, name="w2_s", align_bytes=64)
        wb_w = keep.tile([P, N], U16, name="wb_w", align_bytes=64)
        wb_s = keep.tile([P, N], U8, name="wb_s", align_bytes=64)
        sa_t = keep.tile([P, PACK], F32, name="sa_t")
        sb_t = keep.tile([P, PACK], F32, name="sb_t")
        boards = [keep.tile([P, C], F32, name=f"board{t}") for t in range(PACK)]

        w_s_words = w_s[:].rearrange("p q c -> p (q c)").bitcast(I32)
        nc.vector.memset(xt_s[:].bitcast(I32), 0)
        nc.vector.memset(w_s_words, 0)
        for plane in (w2_s, wb_s):
            nc.vector.memset(plane[:].bitcast(I32), 0)
        for t in range(PACK):
            nc.vector.memset(boards[t][:], 0.0)

        nc.sync.dma_start(out=w_rows[:], in_=w_scales[0].bitcast(I32).rearrange("(q r) c -> r q c", r=4))
        nc.scalar.dma_start(out=xt_w[:].bitcast(I32), in_=xt_words[0].rearrange("p n t -> p (n t)").bitcast(I32))
        load_scale_rows(nc, xt_s, xt_scales)
        nc.sync.dma_start(list1[:], offs)
        nc.sync.dma_start(out=w_w[:].bitcast(I32), in_=w_words[0].bitcast(I32))
        nc.sync.dma_start(list2[:], offs2)
        nc.sync.dma_start(out=w2_w[:].bitcast(I32), in_=w2_words[0].rearrange("p n t -> p (n t)").bitcast(I32))
        load_scale_rows(nc, w2_s, w2_scales)
        nc.sync.dma_start(list3[:], offs3)
        nc.sync.dma_start(out=sa_t[:], in_=sa.rearrange("(p t) one -> p (t one)", t=PACK))
        nc.sync.dma_start(list5[:], offs5)
        nc.sync.dma_start(out=sb_t[:], in_=sb.rearrange("(p t) one -> p (t one)", t=PACK))
        nc.sync.dma_start(list4[:], offs4)
        nc.sync.dma_start(out=wb_w[:].bitcast(I32), in_=wb_words[0].bitcast(I32))
        load_scale_rows(nc, wb_s, wb_scales)

        x_w = keep.tile([P, J], U32, name="x_w", align_bytes=64)
        x_s = keep.tile([P, J], U8, name="x_s", align_bytes=64)
        w_wd = keep.tile([P, R], U16, name="w_wd", align_bytes=64)
        w_sd = keep.tile([P, R], U8, name="w_sd", align_bytes=64)
        w2_wd = keep.tile([P, R], U32, name="w2_wd", align_bytes=64)
        w2_sd = keep.tile([P, R], U8, name="w2_sd", align_bytes=64)

        first_pair, second_pair, all_slices = slice(0, 2), slice(2, PACK), slice(0, PACK)
        for pair in (first_pair, second_pair):
            deal(nc.scalar.copy, w_wd[:], w_w[:], 2, pair)
        by_parity = w_rows[:].rearrange("r (a b) c -> r b a c", b=2)
        for b in range(2):
            nc.vector.tensor_copy(
                out=w_s_words[32 * b : 32 * b + 4, :].rearrange("r (a c) -> r a c", a=2), in_=by_parity[:, b]
            )
        nc.vector.tensor_copy(out=w_s_words[64:128, 0:ROW_WORDS], in_=w_s_words[0:64, ROW_WORDS : 2 * ROW_WORDS])
        for pair in (first_pair, second_pair):
            deal(nc.gpsimd.tensor_copy, w_sd[:], w_s[:, 0, :], 1, pair)
        for lo in (0, HALF):
            slots = entries(list1, lo, lo + HALF)
            nc.vector.tensor_copy(x_s[:, lo : lo + HALF], xt_s[:].indirect(slots))
            nc.vector.tensor_copy(x_w[:, lo : lo + HALF], xt_w[:].indirect(slots))
        deal(nc.gpsimd.tensor_copy, w2_wd[:], w2_w[:], 4, all_slices)
        deal(nc.gpsimd.tensor_copy, w2_sd[:], w2_s[:], 1, all_slices)

        def first_product(dst, t, lo, hi):
            cols = slice(t * P, (t + 1) * P)
            nc.tensor.matmul_mx(
                out=dst, lhsT=w_wd[:, cols].bitcast(E2M1), lhsT_scale=w_sd[:, cols],
                rhs=x_w[:, lo:hi].bitcast(E5M2), rhs_scale=x_s[:, lo:hi], start=True, stop=True,
            )

        early_ps = [psum.tile([P, HALF], F32, name=f"early_ps{t}", tag=f"bank{t}") for t in range(2)]
        for t in range(2):
            first_product(early_ps[t][:], t, 0, HALF)

        early_sb = [keep.tile([P, HALF], F32, name=f"early_sb{t}", tag=f"staged{t}") for t in range(2)]
        picked = [keep.tile([P, J], F32, name=f"picked{t}") for t in range(PACK)]
        rb = [keep.tile([P, J], F32, name=f"rb{t}") for t in range(PACK)]
        other = [keep.tile([P, O], F32, name=f"other{t}") for t in range(PACK)]
        diff = keep.tile([P, PACK, O], F32, name="diff")
        hid = keep.tile([P, O, PACK], BF16, name="hid", align_bytes=64)

        def put_scalar(t, lo, hi, values):
            nc.scalar.activation(out=boards[t][:].indirect(entries(list2, lo, hi)), in_=values, func=ACT.Copy)

        def put_vector(t, lo, hi, values):
            nc.vector.tensor_copy(boards[t][:].indirect(entries(list2, lo, hi)), values)

        nc.scalar.activation(out=early_sb[0][:], in_=early_ps[0][:], func=ACT.Copy)
        nc.vector.tensor_copy(out=early_sb[1][:], in_=early_ps[1][:])
        put_scalar(0, 0, HALF, early_sb[0][:])
        put_vector(1, 0, HALF, early_sb[1][:])

        late_ps = [psum.tile([P, HALF], F32, name=f"late_ps{t}") for t in range(2)]
        a3_ps = psum.tile([P, J], F32, name="a3_ps")
        a2_ps = psum.tile([P, J], F32, name="a2_ps")
        for t in range(2):
            first_product(late_ps[t][:], t, HALF, J)
        first_product(a3_ps[:], 3, 0, J)
        first_product(a2_ps[:], 2, 0, J)

        s_sb = keep.tile([P, HALF + SCALAR_SHARE], F32, name="s_sb", tag="staged0")
        nc.scalar.activation(out=s_sb[:, 0:HALF], in_=late_ps[0][:], func=ACT.Copy)
        nc.scalar.activation(out=s_sb[:, HALF:], in_=a3_ps[:, 0:SCALAR_SHARE], func=ACT.Copy)
        put_scalar(0, HALF, J, s_sb[:, 0:HALF])
        put_scalar(3, 0, SCALAR_SHARE, s_sb[:, HALF:])
        v_sb = keep.tile([P, HALF + 2 * J - SCALAR_SHARE], F32, name="v_sb", tag="staged1")
        nc.vector.tensor_copy(out=v_sb[:, 0:HALF], in_=late_ps[1][:])
        nc.vector.tensor_copy(out=v_sb[:, HALF : HALF + J], in_=a2_ps[:])
        nc.vector.tensor_copy(out=v_sb[:, HALF + J :], in_=a3_ps[:, SCALAR_SHARE:J])
        put_vector(1, HALF, J, v_sb[:, 0:HALF])
        put_vector(2, 0, J, v_sb[:, HALF : HALF + J])
        put_vector(3, SCALAR_SHARE, J, v_sb[:, HALF + J :])

        b_ps = [psum.tile([P, 2, J], F32, name=f"b_ps{h}") for h in range(2)]
        for t in range(PACK):
            cols = slice(t * P, (t + 1) * P)
            nc.tensor.matmul_mx(
                out=b_ps[t // 2][:, t % 2, :], lhsT=w2_wd[:, cols].bitcast(E4M3), lhsT_scale=w2_sd[:, cols],
                rhs=x_w[:].bitcast(E5M2), rhs_scale=x_s[:], start=True, stop=True,
            )

        for t in range(PACK):
            nc.scalar.activation(
                out=picked[t][:], in_=boards[t][:].indirect(list3[:]), func=ACT.Copy, scale=sa_t[:, t : t + 1]
            )
        for t in range(PACK):
            nc.vector.tensor_tensor(out=rb[t][:], in0=picked[t][:], in1=b_ps[t // 2][:, t % 2, :], op=ALU.max)
        for t in range(PACK):
            nc.scalar.activation(
                out=other[t][:], in_=rb[t][:].indirect(list5[:]), func=ACT.Copy, scale=sb_t[:, t : t + 1]
            )
        for t in range(PACK):
            nc.vector.tensor_tensor(out=diff[:, t, :], in0=rb[t][:].indirect(list4[:]), in1=other[t][:], op=ALU.subtract)

        by_place = diff[:].rearrange("p t o -> p o t")
        low, high = slice(0, O // 2), slice(O // 2, O)
        nc.scalar.activation(out=hid[:, :, first_pair], in_=by_place[:, :, first_pair], func=ACT.Abs)
        nc.scalar.activation(out=hid[:, low, second_pair], in_=by_place[:, low, second_pair], func=ACT.Abs)
        nc.vector.scalar_tensor_tensor(
            out=hid[:, high, second_pair], in0=by_place[:, high, second_pair], scalar=-1.0,
            in1=by_place[:, high, second_pair], op0=ALU.mult, op1=ALU.max,
        )

        hid_w = keep.tile([P, O], U32, name="hid_w", align_bytes=64)
        hid_s = keep.tile([P, O], U8, name="hid_s", align_bytes=64)
        nc.vector.quantize_mx(out=hid_w[:].bitcast(E4M3), scales=hid_s[:], in_=hid[:].rearrange("p o t -> p (o t)"))

        y_ps = [psum.tile([P, O], F32, name=f"y_ps{h}", tag=f"bank{h}") for h in range(2)]
        y_sb = [keep.tile([P, O], F32, name=f"y_sb{h}") for h in range(2)]
        for h in range(2):
            cols = slice(h * P, (h + 1) * P)
            nc.tensor.matmul_mx(
                out=y_ps[h][:], lhsT=wb_w[:, cols].bitcast(E2M1), lhsT_scale=wb_s[:, cols],
                rhs=hid_w[:].bitcast(E4M3), rhs_scale=hid_s[:], start=True, stop=True,
            )
        nc.vector.tensor_copy(out=y_sb[0][:], in_=y_ps[0][:])
        nc.sync.dma_start(out=out[0:P, :], in_=y_sb[0][:])
        nc.scalar.copy(out=y_sb[1][:], in_=y_ps[1][:])
        nc.scalar.dma_start(out=out[P : 2 * P, :], in_=y_sb[1][:])
